import numpy as np
import ml_dtypes


def mxq(x, axis, fmt="e4m3"):
    dtype, down = {"e4m3": (ml_dtypes.float8_e4m3fn, 7), "e5m2": (ml_dtypes.float8_e5m2, 14)}[fmt]
    v = np.moveaxis(np.asarray(x, np.float32).astype(ml_dtypes.bfloat16).astype(np.float64), axis, -1)
    blocks = v.reshape(v.shape[:-1] + (-1, 32))
    amax = np.abs(blocks).max(-1, keepdims=True)
    byte = np.maximum(np.where(amax > 0, np.frexp(amax)[1] - 1 + 127, 0) - down, 1)
    scale = np.exp2(byte - 127.0)
    codes = (blocks / scale).astype(np.float32).astype(dtype).astype(np.float64)
    return np.moveaxis((codes * scale).reshape(v.shape), -1, axis)


WIDE = False


def mx_kscale(k):
    if not WIDE:
        return np.ones(k)
    levels = np.array([10, -10, 5, -5, 0])
    if k % 512:
        return np.exp2(np.random.permutation(np.resize(levels, k // 32))).repeat(32)
    a = np.empty((k // 512, 16))
    for p in range(k // 512):
        a[p, :8] = np.random.permutation(np.resize(levels, 8))
        for g in range(8):
            far = levels[np.abs(levels - a[p, g]) >= 10]
            a[p, g + 8] = far[np.random.randint(len(far))]
    return np.exp2(a.ravel()).repeat(32)


BF16 = ml_dtypes.bfloat16


def bf(x):
    return np.asarray(x, np.float32).astype(BF16)


def f64(x):
    return np.asarray(x).astype(np.float64)


E2M1 = np.array([0.0, 0.5, 1.0, 1.5, 2.0, 3.0, 4.0, 6.0, -0.0, -0.5, -1.0, -1.5, -2.0, -3.0, -4.0, -6.0])


def pack_weight(w, fmt):
    k, n = w.shape
    w = f64(bf(w)).reshape(k // 32, 32, n)
    amax = np.abs(w).max(1)
    if fmt == "e4m3":
        byte = np.frexp(amax)[1] - 1 + 127 - 7
    else:
        mant, ex = np.frexp(amax / 6.0)
        byte = np.where(mant > 0.5, ex, ex - 1) + 127
    byte = np.clip(np.where(amax > 0, byte, 1), 1, 254)
    scaled = (w * np.exp2(127.0 - byte)[:, None, :]).reshape(k, n).astype(np.float32)
    by_word = np.ascontiguousarray(scaled.reshape(k // 512, 128, 4, n).transpose(0, 1, 3, 2))
    if fmt == "e4m3":
        words = by_word.astype(ml_dtypes.float8_e4m3fn).view(np.uint8)
    else:
        c = by_word.astype(ml_dtypes.float4_e2m1fn).view(np.uint8) & 0xF
        words = c[..., 0::2] | (c[..., 1::2] << 4)
    return np.ascontiguousarray(words), np.ascontiguousarray(byte.astype(np.uint8).reshape(k // 512, 16, n))


def unpack_weight(words, scales, fmt):
    g, p, n, _ = words.shape
    if fmt == "e4m3":
        vals = np.ascontiguousarray(words).view(ml_dtypes.float8_e4m3fn).astype(np.float64)
    else:
        nib = np.empty((g, p, n, 4), np.uint8)
        nib[..., 0::2] = words & 0xF
        nib[..., 1::2] = words >> 4
        vals = E2M1[nib]
    vals = vals * np.repeat(np.exp2(scales.astype(np.float64) - 127.0), 8, axis=1)[..., None]
    return vals.transpose(0, 1, 3, 2).reshape(g * 512, n)


N, D, R, O = 1024, 1024, 1024, 1024


def draw0():
    s, t = mx_kscale(D), mx_kscale(R)
    z = bf(np.random.standard_normal((N, D)) * s)
    u1_words, u1_scales = pack_weight(np.random.standard_normal((D, R)) / np.sqrt(D) / s[:, None] * t, "e4m3")
    u2_words, u2_scales = pack_weight(np.random.standard_normal((D, R)) / np.sqrt(D) / s[:, None], "e4m3")
    u3_words, u3_scales = pack_weight(np.random.standard_normal((D, R)) / np.sqrt(D) / s[:, None], "e4m3")
    c_words, c_scales = pack_weight(np.random.standard_normal((R, O)) / np.sqrt(R) / t[:, None], "e4m3")
    return {
        "z": z,
        "u1_words": u1_words,
        "u1_scales": u1_scales,
        "u2_words": u2_words,
        "u2_scales": u2_scales,
        "u3_words": u3_words,
        "u3_scales": u3_scales,
        "c_words": c_words,
        "c_scales": c_scales,
        "beta": bf(0.3 * np.random.standard_normal(O)),
    }


def raise_degree(a, x):
    return a * x + x


def core(z, u1_words, u1_scales, u2_words, u2_scales, u3_words, u3_scales, c_words, c_scales, beta):
    zq = mxq(f64(z), 1, "e4m3")
    x1 = zq @ unpack_weight(u1_words, u1_scales, "e4m3")
    a2 = zq @ unpack_weight(u2_words, u2_scales, "e4m3")
    a3 = zq @ unpack_weight(u3_words, u3_scales, "e4m3")
    x2 = raise_degree(a2, x1)
    x3 = raise_degree(a3, x2)
    return (mxq(x3, 1, "e4m3") @ unpack_weight(c_words, c_scales, "e4m3")) + f64(beta)[None, :]


def e4m3fn_bytes(y):
    return np.clip(np.asarray(y, np.float64), -448.0, 448.0).astype(np.float32).astype(ml_dtypes.float8_e4m3fn).view(np.uint8)


def e4m3fn_values(b):
    return np.asarray(b, np.uint8).view(ml_dtypes.float8_e4m3fn).astype(np.float64)


def setup_inputs():
    d = draw0()
    x0 = np.asarray(d['z']).astype(np.float64)
    s = (np.max(np.abs(x0), axis=(0,), keepdims=True) / 448.0).astype(np.float32)
    out = {}
    for k, v in d.items():
        if k == 'z':
            out['z_bytes'] = e4m3fn_bytes(x0 / s.astype(np.float64))
            out['z_scale'] = s
        else:
            out[k] = v
    return out


def reference(z_bytes, z_scale, u1_words, u1_scales, u2_words, u2_scales, u3_words, u3_scales, c_words, c_scales, beta):
    return core(e4m3fn_values(z_bytes) * z_scale.astype(np.float64), u1_words, u1_scales, u2_words, u2_scales, u3_words, u3_scales, c_words, c_scales, beta)

@@ -1,0 +1,293 @@
+from contextlib import ExitStack
+
+import concourse.mybir as mybir
+from concourse.masks import make_identity
+
+N, D, R, O = 1024, 1024, 1024, 1024
+FLOPS = 2 * N * D * R * 3 + 2 * N * R * O
+
+F32 = mybir.dt.float32
+BF16 = mybir.dt.bfloat16
+U32 = mybir.dt.uint32
+I32 = mybir.dt.int32
+U8 = mybir.dt.uint8
+FP8 = mybir.dt.float8_e4m3fn
+FP8X4 = mybir.dt.float8_e4m3fn_x4
+ALU = mybir.AluOpType
+ACT = mybir.ActivationFunctionType
+
+P = 128
+TILES = N // P
+HALF = 512
+GROUPS = 2
+
+
+def tile_pinetccpthirddegreepolynomial_w8_kernel(
+    tc, z_bytes, z_scale, u1_words, u1_scales, u2_words, u2_scales, u3_words, u3_scales, c_words, c_scales, beta, out
+):
+    nc = tc.nc
+    words_in = {"u1": u1_words, "u2": u2_words, "u3": u3_words, "c": c_words}
+    scales_in = {"u1": u1_scales, "u2": u2_scales, "u3": u3_scales, "c": c_scales}
+    first_row = {"u2": 0, "u3": 8, "u1": 0, "c": 8}
+    z_rows = z_bytes.rearrange("(p j) k -> p j k", j=TILES)
+    out_rows = out.rearrange("(p j) o -> p j o", j=TILES)
+
+    with ExitStack() as ctx:
+        keep = ctx.enter_context(tc.tile_pool(name="keep", bufs=1))
+        work = ctx.enter_context(tc.tile_pool(name="work", bufs=3))
+        psum = ctx.enter_context(tc.psum_pool(name="psum", bufs=1))
+        ctx.enter_context(tc.manual_schedule())
+
+        ident = keep.tile([P, P], F32, name="ident")
+        make_identity(nc, ident[:])
+
+        w_codes = {}
+        w_scales = {}
+        for w in ("u2", "u3", "u1", "c"):
+            w_scales[w] = keep.tile([P, R], U8, name="scales_" + w, align_bytes=64)
+            nc.vector.memset(w_scales[w][:].bitcast(I32), 0)
+            for h in range(2):
+                w_codes[w, h] = keep.tile([P, GROUPS, HALF], U32, name="codes_%s_%d" % (w, h), align_bytes=64)
+
+        z_raw = {}
+
+        def load_z(first, count):
+            t = keep.tile([P, count * D], U8, name="z_raw_%d" % first, align_bytes=64)
+            nc.sync.dma_start(out=t[:], in_=z_rows[:, first : first + count, :].rearrange("p j k -> p (j k)"))
+            for j in range(count):
+                z_raw[first + j] = t[:, j * D : (j + 1) * D]
+
+        def load_scales(w):
+            for q in range(4):
+                row = 32 * q + first_row[w]
+                nc.sync.dma_start(
+                    out=w_scales[w][row : row + 8, :].bitcast(I32),
+                    in_=scales_in[w][:, 4 * q : 4 * q + 4, :].bitcast(I32),
+                )
+
+        def load_codes(w, h):
+            src = words_in[w].rearrange("g p n t -> p g (n t)")[:, :, 4 * HALF * h : 4 * HALF * (h + 1)]
+            nc.sync.dma_start(out=w_codes[w, h][:].bitcast(I32), in_=src.bitcast(I32))
+
+        zs = keep.tile([P, GROUPS, 4], F32, name="zs")
+        beta_sb = keep.tile([P, O], BF16, name="beta_sb")
+
+        load_z(0, 1)
+        load_z(1, 1)
+        nc.sync.dma_start(out=zs[:], in_=z_scale.rearrange("o (g p t) -> p (o g) t", p=P, t=4))
+        load_scales("u2")
+        load_codes("u2", 0)
+        load_z(2, 1)
+        load_scales("u3")
+        load_codes("u3", 0)
+        load_scales("u1")
+        load_codes("u1", 0)
+        load_z(3, 1)
+        load_codes("u2", 1)
+        load_codes("u3", 1)
+        load_codes("u1", 1)
+        load_z(4, 4)
+        load_scales("c")
+        load_codes("c", 0)
+        load_codes("c", 1)
+        nc.sync.dma_start(out=beta_sb[:], in_=beta.partition_broadcast(P))
+
+        z_wide, z_turned, z_grouped, z_codes, z_scales = {}, {}, {}, {}, {}
+        x3, x3_grouped, x3_codes, x3_scales, acc = {}, {}, {}, {}, {}
+
+        def widen_z(i, g, copy):
+            z_wide[i, g] = work.tile([P, HALF], BF16, name="z_wide", bufs=6, align_bytes=64)
+            copy(out=z_wide[i, g][:], in_=z_raw[i][:, g * HALF : (g + 1) * HALF].bitcast(FP8))
+
+        def turn_z(i, groups):
+            bank = psum.tile([P, 4, P], F32, name="turned", bufs=2)
+            for g in groups:
+                z_turned[i, g] = bank
+                words = z_wide[i, g][:].bitcast(F32)
+                for u in range(2):
+                    nc.tensor.transpose(bank[:, 2 * g + u, :], words[:, u : 256 : 2], ident[:])
+
+        def scale_z(i, g):
+            z_grouped[i, g] = work.tile([P, HALF], BF16, name="z_grouped", bufs=4, align_bytes=64)
+            src = z_turned[i, g][:].rearrange("p a n -> p (a n)").bitcast(BF16)
+            src = src[:, g * HALF : (g + 1) * HALF].rearrange("p (u n e) -> p n u e", u=2, e=2)
+            factor = zs[:, g, :].rearrange("p (u e) -> p u e", u=2).unsqueeze(1).to_broadcast([P, P, 2, 2])
+            dst = z_grouped[i, g][:].rearrange("p (n u e) -> p n u e", u=2, e=2)
+            nc.vector.tensor_tensor(out=dst, in0=src, in1=factor, op=ALU.mult)
+
+        def quantize_z(i, g):
+            z_codes[i, g] = work.tile([P, P], U32, name="z_codes", bufs=8, align_bytes=64)
+            z_scales[i, g] = work.tile([P, P], U8, name="z_scales", bufs=8, align_bytes=64)
+            nc.vector.quantize_mx(out=z_codes[i, g][:].bitcast(FP8X4), scales=z_scales[i, g][:], in_=z_grouped[i, g][:])
+
+        def mx_pass(dst, codes, scales, w, h, g):
+            row = first_row[w] + 4 * g
+            nc.tensor.matmul_mx(
+                out=dst,
+                lhsT=codes.bitcast(FP8X4),
+                lhsT_scale=scales,
+                rhs=w_codes[w, h][:, g, :].bitcast(FP8X4),
+                rhs_scale=w_scales[w][row:P, h * HALF : (h + 1) * HALF],
+                start=(g == 0),
+                stop=(g == GROUPS - 1),
+            )
+
+        def linear_form(i, w, h):
+            bank = psum.tile([P, HALF], F32, name="form", bufs=4)
+            for g in range(GROUPS):
+                mx_pass(bank[:], z_codes[i, g][:], z_scales[i, g][:], w, h, g)
+            return bank
+
+        b2, y = {}, {}
+
+        def step_a2(i, h):
+            bank = linear_form(i, "u2", h)
+            b2[i, h] = work.tile([P, HALF], F32, name="b2")
+            nc.scalar.activation(out=b2[i, h][:], in_=bank[:], func=ACT.Copy, bias=1.0)
+
+        def step_a3(i, h):
+            bank = linear_form(i, "u3", h)
+            y[i, h] = work.tile([P, HALF], F32, name="y")
+            nc.vector.scalar_tensor_tensor(
+                out=y[i, h][:], in0=bank[:], scalar=1.0, in1=b2[i, h][:], op0=ALU.add, op1=ALU.mult
+            )
+
+        def step_x1(i, h):
+            bank = linear_form(i, "u1", h)
+            x3[i, h] = work.tile([P, HALF], BF16, name="x3", bufs=4, align_bytes=64)
+            nc.vector.tensor_tensor(
+                out=x3[i, h][:].rearrange("n (u p e) -> n u p e", u=2, e=2),
+                in0=bank[:].rearrange("n (p u e) -> n u p e", u=2, e=2),
+                in1=y[i, h][:].rearrange("n (p u e) -> n u p e", u=2, e=2),
+                op=ALU.mult,
+            )
+
+        def turn_x3(i, groups):
+            count = len(groups)
+            turned = psum.tile([P, 4, P], F32, name="turned", bufs=2)
+            for j, g in enumerate(groups):
+                words = x3[i, g][:].bitcast(F32)
+                for u in range(2):
+                    nc.tensor.transpose(turned[:, 2 * j + u, :], words[:, u * P : (u + 1) * P], ident[:])
+            grouped = work.tile([P, count * HALF], BF16, name="x3_grouped", align_bytes=64)
+            x3_grouped[i, groups[0]] = grouped
+            nc.scalar.copy(
+                out=grouped[:].bitcast(F32).rearrange("p (g n u) -> p g n u", g=count, u=2),
+                in_=turned[:, 0 : 2 * count, :].rearrange("p (g u) n -> p g n u", u=2),
+            )
+
+        def quantize_x3(i, groups):
+            count = len(groups)
+            codes = work.tile([P, count * P], U32, name="x3_codes", bufs=4, align_bytes=64)
+            scales = work.tile([P, count * P], U8, name="x3_scales", bufs=4, align_bytes=64)
+            nc.vector.quantize_mx(out=codes[:].bitcast(FP8X4), scales=scales[:], in_=x3_grouped[i, groups[0]][:])
+            for j, g in enumerate(groups):
+                x3_codes[i, g] = codes[:, j * P : (j + 1) * P]
+                x3_scales[i, g] = scales[:, j * P : (j + 1) * P]
+
+        def project(i, tag, banks):
+            for h in range(2):
+                acc[i, h] = psum.tile([P, HALF], F32, name=tag, bufs=banks)
+                for g in range(GROUPS):
+                    mx_pass(acc[i, h][:], x3_codes[i, g], x3_scales[i, g], "c", h, g)
+
+        def finish(i, h):
+            res = work.tile([P, HALF], F32, name="res", bufs=6)
+            cols = slice(h * HALF, (h + 1) * HALF)
+            nc.vector.tensor_tensor(out=res[:], in0=acc[i, h][:], in1=beta_sb[:, cols], op=ALU.add)
+            nc.sync.dma_start(out=out_rows[:, i, cols], in_=res[:])
+
+        both = [0, 1]
+        widen_z(0, 0, nc.vector.tensor_copy)
+        widen_z(0, 1, nc.scalar.copy)
+        widen_z(1, 0, nc.vector.tensor_copy)
+        widen_z(1, 1, nc.scalar.copy)
+        turn_z(0, both)
+        turn_z(1, both)
+        for g in both:
+            widen_z(2, g, nc.scalar.copy)
+        scale_z(0, 0)
+        scale_z(0, 1)
+        quantize_z(0, 0)
+        scale_z(1, 0)
+        quantize_z(0, 1)
+        scale_z(1, 1)
+        turn_z(2, both)
+        step_a2(0, 0)
+        quantize_z(1, 0)
+        scale_z(2, 0)
+        quantize_z(1, 1)
+        step_a3(0, 0)
+        step_a2(1, 0)
+        for g in both:
+            widen_z(3, g, nc.scalar.copy)
+        scale_z(2, 1)
+        step_a3(1, 0)
+        step_x1(0, 0)
+        quantize_z(2, 0)
+        quantize_z(2, 1)
+        step_x1(1, 0)
+        turn_z(3, both)
+        step_a2(0, 1)
+        for g in both:
+            widen_z(4, g, nc.scalar.copy)
+        step_a3(0, 1)
+        scale_z(3, 0)
+        step_x1(0, 1)
+        step_a2(1, 1)
+        scale_z(3, 1)
+        step_a3(1, 1)
+        for g in both:
+            quantize_z(3, g)
+        step_x1(1, 1)
+        turn_x3(0, both)
+
+        last = TILES - 1
+        for i in range(2, last):
+            ahead = i + 2
+            step_a2(i, 0)
+            step_a3(i, 0)
+            if i == 2:
+                quantize_x3(0, both)
+            else:
+                finish(i - 3, 1)
+            step_x1(i, 0)
+            turn_x3(i - 1, both)
+            if ahead < TILES:
+                turn_z(ahead, both)
+                scale_z(ahead, 0)
+            quantize_x3(i - 1, both)
+            if ahead < TILES:
+                scale_z(ahead, 1)
+            step_a2(i, 1)
+            if ahead + 1 < TILES:
+                for g in both:
+                    widen_z(ahead + 1, g, nc.scalar.copy)
+            step_a3(i, 1)
+            if ahead < TILES:
+                for g in both:
+                    quantize_z(ahead, g)
+            step_x1(i, 1)
+            project(i - 2, "acc", 2)
+            finish(i - 2, 0)
+        step_a2(last, 0)
+        step_a3(last, 0)
+        finish(last - 3, 1)
+        step_x1(last, 0)
+        step_a2(last, 1)
+        step_a3(last, 1)
+        turn_x3(last - 1, both)
+        turn_x3(last, [0])
+        quantize_x3(last - 1, both)
+        step_x1(last, 1)
+        project(last - 2, "acc", 2)
+        quantize_x3(last, [0])
+        finish(last - 2, 0)
+        turn_x3(last, [1])
+        finish(last - 2, 1)
+        project(last - 1, "form", 4)
+        quantize_x3(last, [1])
+        project(last, "form", 4)
+        for i in (last - 1, last):
+            for h in range(2):
+                finish(i, h)

@@ -20,6 +20,7 @@ P = 128
 TILES = N // P
 HALF = 512
 GROUPS = 2
+FORM_BANKS = 4
 
 
 def tile_pinetccpthirddegreepolynomial_w8_kernel(
@@ -73,11 +74,10 @@ def tile_pinetccpthirddegreepolynomial_w8_kernel(
         beta_sb = keep.tile([P, O], BF16, name="beta_sb")
 
         load_z(0, 1)
-        load_z(1, 1)
+        load_z(1, 2)
         nc.sync.dma_start(out=zs[:], in_=z_scale.rearrange("o (g p t) -> p (o g) t", p=P, t=4))
         load_scales("u2")
         load_codes("u2", 0)
-        load_z(2, 1)
         load_scales("u3")
         load_codes("u3", 0)
         load_scales("u1")
@@ -92,20 +92,36 @@ def tile_pinetccpthirddegreepolynomial_w8_kernel(
         load_codes("c", 1)
         nc.sync.dma_start(out=beta_sb[:], in_=beta.partition_broadcast(P))
 
+        z_words = {}
         z_wide, z_turned, z_grouped, z_codes, z_scales = {}, {}, {}, {}, {}
         x3, x3_grouped, x3_codes, x3_scales, acc = {}, {}, {}, {}, {}
 
-        def widen_z(i, g, copy):
-            z_wide[i, g] = work.tile([P, HALF], BF16, name="z_wide", bufs=6, align_bytes=64)
-            copy(out=z_wide[i, g][:], in_=z_raw[i][:, g * HALF : (g + 1) * HALF].bitcast(FP8))
+        def widen_half(i, g, copy):
+            wide = work.tile([P, HALF], BF16, name="z_first", bufs=6, align_bytes=64)
+            copy(out=wide[:], in_=z_raw[i][:, g * HALF : (g + 1) * HALF].bitcast(FP8))
+            for u in range(2):
+                z_words[i, g, u] = wide[:].bitcast(F32)[:, u : 256 : 2]
 
-        def turn_z(i, groups):
-            bank = psum.tile([P, 4, P], F32, name="turned", bufs=2)
+        def widen_z(i):
+            z_wide[i] = work.tile([P, D], BF16, name="z_wide", bufs=2, align_bytes=64)
+            nc.scalar.copy(out=z_wide[i][:], in_=z_raw[i].bitcast(FP8))
+
+        def sort_z(i):
+            sorted_words = work.tile([P, GROUPS * 2 * P], F32, name="z_sorted", bufs=2, align_bytes=64)
+            nc.scalar.copy(
+                out=sorted_words[:].rearrange("n (g u p) -> n g u p", g=GROUPS, u=2),
+                in_=z_wide[i][:].bitcast(F32).rearrange("n (g p u) -> n g u p", g=GROUPS, u=2),
+            )
+            for g in range(GROUPS):
+                for u in range(2):
+                    z_words[i, g, u] = sorted_words[:, (2 * g + u) * P : (2 * g + u + 1) * P]
+
+        def turn_z(i, groups, tag="turned"):
+            bank = psum.tile([P, 4, P], F32, name=tag, bufs=2)
             for g in groups:
                 z_turned[i, g] = bank
-                words = z_wide[i, g][:].bitcast(F32)
                 for u in range(2):
-                    nc.tensor.transpose(bank[:, 2 * g + u, :], words[:, u : 256 : 2], ident[:])
+                    nc.tensor.transpose(bank[:, 2 * g + u, :], z_words[i, g, u], ident[:])
 
         def scale_z(i, g):
             z_grouped[i, g] = work.tile([P, HALF], BF16, name="z_grouped", bufs=4, align_bytes=64)
@@ -133,7 +149,7 @@ def tile_pinetccpthirddegreepolynomial_w8_kernel(
             )
 
         def linear_form(i, w, h):
-            bank = psum.tile([P, HALF], F32, name="form", bufs=4)
+            bank = psum.tile([P, HALF], F32, name="form", bufs=FORM_BANKS)
             for g in range(GROUPS):
                 mx_pass(bank[:], z_codes[i, g][:], z_scales[i, g][:], w, h, g)
             return bank
@@ -198,57 +214,57 @@ def tile_pinetccpthirddegreepolynomial_w8_kernel(
             nc.sync.dma_start(out=out_rows[:, i, cols], in_=res[:])
 
         both = [0, 1]
-        widen_z(0, 0, nc.vector.tensor_copy)
-        widen_z(0, 1, nc.scalar.copy)
-        widen_z(1, 0, nc.vector.tensor_copy)
-        widen_z(1, 1, nc.scalar.copy)
-        turn_z(0, both)
-        turn_z(1, both)
-        for g in both:
-            widen_z(2, g, nc.scalar.copy)
-        scale_z(0, 0)
-        scale_z(0, 1)
-        quantize_z(0, 0)
-        scale_z(1, 0)
-        quantize_z(0, 1)
-        scale_z(1, 1)
-        turn_z(2, both)
+        widen_half(0, 0, nc.vector.tensor_copy)
+        widen_half(0, 1, nc.scalar.copy)
+        widen_half(1, 0, nc.vector.tensor_copy)
+        widen_half(1, 1, nc.scalar.copy)
+        widen_half(2, 0, nc.scalar.copy)
+        widen_half(2, 1, nc.scalar.copy)
+        turn_z(0, [0])
+        turn_z(0, [1])
+        turn_z(1, both, "acc")
+        turn_z(2, both, "acc")
+        for i in range(2):
+            for g in both:
+                scale_z(i, g)
+            for g in both:
+                quantize_z(i, g)
         step_a2(0, 0)
-        quantize_z(1, 0)
         scale_z(2, 0)
-        quantize_z(1, 1)
         step_a3(0, 0)
         step_a2(1, 0)
-        for g in both:
-            widen_z(3, g, nc.scalar.copy)
         scale_z(2, 1)
         step_a3(1, 0)
         step_x1(0, 0)
-        quantize_z(2, 0)
-        quantize_z(2, 1)
+        widen_z(3)
         step_x1(1, 0)
-        turn_z(3, both)
         step_a2(0, 1)
-        for g in both:
-            widen_z(4, g, nc.scalar.copy)
-        step_a3(0, 1)
-        scale_z(3, 0)
-        step_x1(0, 1)
+        sort_z(3)
         step_a2(1, 1)
-        scale_z(3, 1)
-        step_a3(1, 1)
+        step_a3(0, 1)
+        widen_z(4)
         for g in both:
-            quantize_z(3, g)
+            quantize_z(2, g)
+        step_x1(0, 1)
+        step_a3(1, 1)
         step_x1(1, 1)
+        sort_z(4)
         turn_x3(0, both)
+        turn_z(3, both)
+        for g in both:
+            scale_z(3, g)
 
         last = TILES - 1
         for i in range(2, last):
             ahead = i + 2
             step_a2(i, 0)
+            if ahead + 1 < TILES:
+                widen_z(ahead + 1)
             step_a3(i, 0)
             if i == 2:
                 quantize_x3(0, both)
+                for g in both:
+                    quantize_z(3, g)
             else:
                 finish(i - 3, 1)
             step_x1(i, 0)
@@ -261,8 +277,7 @@ def tile_pinetccpthirddegreepolynomial_w8_kernel(
                 scale_z(ahead, 1)
             step_a2(i, 1)
             if ahead + 1 < TILES:
-                for g in both:
-                    widen_z(ahead + 1, g, nc.scalar.copy)
+                sort_z(ahead + 1)
             step_a3(i, 1)
             if ahead < TILES:
                 for g in both:
@@ -285,9 +300,9 @@ def tile_pinetccpthirddegreepolynomial_w8_kernel(
         finish(last - 2, 0)
         turn_x3(last, [1])
         finish(last - 2, 1)
-        project(last - 1, "form", 4)
+        project(last - 1, "form", FORM_BANKS)
         quantize_x3(last, [1])
-        project(last, "form", 4)
+        project(last, "form", FORM_BANKS)
         for i in (last - 1, last):
             for h in range(2):
                 finish(i, h)

@@ -4,7 +4,7 @@ import concourse.mybir as mybir
 from concourse.masks import make_identity
 
 N, D, R, O = 1024, 1024, 1024, 1024
-FLOPS = 2 * N * D * R * 3 + 2 * N * R * O
+FLOPS = 3 * 2 * N * D * R + 2 * N * R * O
 
 F32 = mybir.dt.float32
 BF16 = mybir.dt.bfloat16
@@ -18,9 +18,13 @@ ACT = mybir.ActivationFunctionType
 
 P = 128
 TILES = N // P
-HALF = 512
-GROUPS = 2
-FORM_BANKS = 4
+GROUP = 512
+BANK = 512
+BOTH = [0, 1]
+HEAD = 3
+FORM_BANKS, ACC_BANKS, TURN_BANKS = 4, 2, 2
+BANKS = {"form": FORM_BANKS, "acc": ACC_BANKS, "turned": TURN_BANKS}
+SCALE_ROW = {"u2": 0, "u3": 8, "u1": 0, "c": 8}
 
 
 def tile_pinetccpthirddegreepolynomial_w8_kernel(
@@ -29,9 +33,8 @@ def tile_pinetccpthirddegreepolynomial_w8_kernel(
     nc = tc.nc
     words_in = {"u1": u1_words, "u2": u2_words, "u3": u3_words, "c": c_words}
     scales_in = {"u1": u1_scales, "u2": u2_scales, "u3": u3_scales, "c": c_scales}
-    first_row = {"u2": 0, "u3": 8, "u1": 0, "c": 8}
-    z_rows = z_bytes.rearrange("(p j) k -> p j k", j=TILES)
-    out_rows = out.rearrange("(p j) o -> p j o", j=TILES)
+    z_rows = z_bytes.rearrange("(n i) k -> n i k", i=TILES)
+    out_rows = out.rearrange("(n i) o -> n i o", i=TILES)
 
     with ExitStack() as ctx:
         keep = ctx.enter_context(tc.tile_pool(name="keep", bufs=1))
@@ -42,154 +45,159 @@ def tile_pinetccpthirddegreepolynomial_w8_kernel(
         ident = keep.tile([P, P], F32, name="ident")
         make_identity(nc, ident[:])
 
-        w_codes = {}
-        w_scales = {}
+        zeros = keep.tile([P, BANK], BF16, name="zeros", align_bytes=64)
+        nc.vector.memset(zeros[:], 0.0)
+
+        def warm_up(count):
+            bank = psum.tile([P, BANK], F32, name="form", bufs=FORM_BANKS)
+            for j in range(count):
+                nc.tensor.matmul(bank[:], lhsT=zeros[:, 0:P], rhs=zeros[:], start=True, stop=True)
+
+        warm_up(3)
+
+        w_codes, w_scales, z_raw = {}, {}, {}
         for w in ("u2", "u3", "u1", "c"):
             w_scales[w] = keep.tile([P, R], U8, name="scales_" + w, align_bytes=64)
             nc.vector.memset(w_scales[w][:].bitcast(I32), 0)
-            for h in range(2):
-                w_codes[w, h] = keep.tile([P, GROUPS, HALF], U32, name="codes_%s_%d" % (w, h), align_bytes=64)
-
-        z_raw = {}
+            for h in BOTH:
+                w_codes[w, h] = keep.tile([P, len(BOTH), BANK], U32, name="codes_%s_%d" % (w, h), align_bytes=64)
 
         def load_z(first, count):
-            t = keep.tile([P, count * D], U8, name="z_raw_%d" % first, align_bytes=64)
-            nc.sync.dma_start(out=t[:], in_=z_rows[:, first : first + count, :].rearrange("p j k -> p (j k)"))
+            raw = keep.tile([P, count * D], U8, name="z_raw_%d" % first, align_bytes=64)
+            nc.sync.dma_start(out=raw[:], in_=z_rows[:, first : first + count, :].rearrange("n i k -> n (i k)"))
             for j in range(count):
-                z_raw[first + j] = t[:, j * D : (j + 1) * D]
+                z_raw[first + j] = raw[:, j * D : (j + 1) * D]
 
         def load_scales(w):
             for q in range(4):
-                row = 32 * q + first_row[w]
+                row = 32 * q + SCALE_ROW[w]
                 nc.sync.dma_start(
                     out=w_scales[w][row : row + 8, :].bitcast(I32),
                     in_=scales_in[w][:, 4 * q : 4 * q + 4, :].bitcast(I32),
                 )
 
         def load_codes(w, h):
-            src = words_in[w].rearrange("g p n t -> p g (n t)")[:, :, 4 * HALF * h : 4 * HALF * (h + 1)]
+            src = words_in[w].rearrange("g p n t -> p g (n t)")[:, :, 4 * BANK * h : 4 * BANK * (h + 1)]
             nc.sync.dma_start(out=w_codes[w, h][:].bitcast(I32), in_=src.bitcast(I32))
 
-        zs = keep.tile([P, GROUPS, 4], F32, name="zs")
-        beta_sb = keep.tile([P, O], BF16, name="beta_sb")
+        z_factor = keep.tile([P, len(BOTH), 4], F32, name="z_factor")
+        beta_all = keep.tile([P, O], BF16, name="beta_all")
 
         load_z(0, 1)
-        load_z(1, 2)
-        nc.sync.dma_start(out=zs[:], in_=z_scale.rearrange("o (g p t) -> p (o g) t", p=P, t=4))
-        load_scales("u2")
-        load_codes("u2", 0)
-        load_scales("u3")
-        load_codes("u3", 0)
+        load_z(1, HEAD - 1)
+        nc.sync.dma_start(out=z_factor[:], in_=z_scale.rearrange("o (g p t) -> p (o g) t", p=P, t=4))
+        for w, tile in (("u2", HEAD), ("u3", HEAD + 1)):
+            load_scales(w)
+            load_codes(w, 0)
+            load_z(tile, 1)
+            load_codes(w, 1)
         load_scales("u1")
-        load_codes("u1", 0)
-        load_z(3, 1)
-        load_codes("u2", 1)
-        load_codes("u3", 1)
-        load_codes("u1", 1)
-        load_z(4, 4)
+        for h in BOTH:
+            load_codes("u1", h)
+        load_z(HEAD + 2, TILES - HEAD - 2)
         load_scales("c")
-        load_codes("c", 0)
-        load_codes("c", 1)
-        nc.sync.dma_start(out=beta_sb[:], in_=beta.partition_broadcast(P))
+        for h in BOTH:
+            load_codes("c", h)
+        nc.sync.dma_start(out=beta_all[:], in_=beta.partition_broadcast(P))
 
-        z_words = {}
-        z_wide, z_turned, z_grouped, z_codes, z_scales = {}, {}, {}, {}, {}
-        x3, x3_grouped, x3_codes, x3_scales, acc = {}, {}, {}, {}, {}
+        z_wide, z_words, z_turned, z_grouped, z_codes, z_scales = {}, {}, {}, {}, {}, {}
 
-        def widen_half(i, g, copy):
-            wide = work.tile([P, HALF], BF16, name="z_first", bufs=6, align_bytes=64)
-            copy(out=wide[:], in_=z_raw[i][:, g * HALF : (g + 1) * HALF].bitcast(FP8))
+        def widen_group(i, g, copy):
+            wide = work.tile([P, GROUP], BF16, name="z_first", bufs=2 * HEAD, align_bytes=64)
+            copy(out=wide[:], in_=z_raw[i][:, g * GROUP : (g + 1) * GROUP].bitcast(FP8))
             for u in range(2):
-                z_words[i, g, u] = wide[:].bitcast(F32)[:, u : 256 : 2]
+                z_words[i, g, u] = wide[:].bitcast(F32)[:, u : GROUP // 2 : 2]
 
         def widen_z(i):
             z_wide[i] = work.tile([P, D], BF16, name="z_wide", bufs=2, align_bytes=64)
             nc.scalar.copy(out=z_wide[i][:], in_=z_raw[i].bitcast(FP8))
 
         def sort_z(i):
-            sorted_words = work.tile([P, GROUPS * 2 * P], F32, name="z_sorted", bufs=2, align_bytes=64)
+            ordered = work.tile([P, D // 2], F32, name="z_sorted", bufs=2, align_bytes=64)
             nc.scalar.copy(
-                out=sorted_words[:].rearrange("n (g u p) -> n g u p", g=GROUPS, u=2),
-                in_=z_wide[i][:].bitcast(F32).rearrange("n (g p u) -> n g u p", g=GROUPS, u=2),
+                out=ordered[:].rearrange("n (g u p) -> n g u p", g=2, u=2),
+                in_=z_wide[i][:].bitcast(F32).rearrange("n (g p u) -> n g u p", g=2, u=2),
             )
-            for g in range(GROUPS):
+            for g in BOTH:
                 for u in range(2):
-                    z_words[i, g, u] = sorted_words[:, (2 * g + u) * P : (2 * g + u + 1) * P]
+                    z_words[i, g, u] = ordered[:, (2 * g + u) * P : (2 * g + u + 1) * P]
 
         def turn_z(i, groups, tag="turned"):
-            bank = psum.tile([P, 4, P], F32, name=tag, bufs=2)
+            bank = psum.tile([P, 4, P], F32, name=tag, bufs=BANKS[tag])
             for g in groups:
                 z_turned[i, g] = bank
                 for u in range(2):
                     nc.tensor.transpose(bank[:, 2 * g + u, :], z_words[i, g, u], ident[:])
 
         def scale_z(i, g):
-            z_grouped[i, g] = work.tile([P, HALF], BF16, name="z_grouped", bufs=4, align_bytes=64)
-            src = z_turned[i, g][:].rearrange("p a n -> p (a n)").bitcast(BF16)
-            src = src[:, g * HALF : (g + 1) * HALF].rearrange("p (u n e) -> p n u e", u=2, e=2)
-            factor = zs[:, g, :].rearrange("p (u e) -> p u e", u=2).unsqueeze(1).to_broadcast([P, P, 2, 2])
-            dst = z_grouped[i, g][:].rearrange("p (n u e) -> p n u e", u=2, e=2)
-            nc.vector.tensor_tensor(out=dst, in0=src, in1=factor, op=ALU.mult)
-
-        def quantize_z(i, g):
-            z_codes[i, g] = work.tile([P, P], U32, name="z_codes", bufs=8, align_bytes=64)
-            z_scales[i, g] = work.tile([P, P], U8, name="z_scales", bufs=8, align_bytes=64)
-            nc.vector.quantize_mx(out=z_codes[i, g][:].bitcast(FP8X4), scales=z_scales[i, g][:], in_=z_grouped[i, g][:])
-
-        def mx_pass(dst, codes, scales, w, h, g):
-            row = first_row[w] + 4 * g
-            nc.tensor.matmul_mx(
-                out=dst,
-                lhsT=codes.bitcast(FP8X4),
-                lhsT_scale=scales,
-                rhs=w_codes[w, h][:, g, :].bitcast(FP8X4),
-                rhs_scale=w_scales[w][row:P, h * HALF : (h + 1) * HALF],
-                start=(g == 0),
-                stop=(g == GROUPS - 1),
+            z_grouped[i, g] = work.tile([P, GROUP], BF16, name="z_grouped", bufs=4, align_bytes=64)
+            values = z_turned[i, g][:].rearrange("p a n -> p (a n)").bitcast(BF16)
+            values = values[:, g * GROUP : (g + 1) * GROUP].rearrange("p (u n e) -> p n u e", u=2, e=2)
+            factor = z_factor[:, g, :].rearrange("p (u e) -> p u e", u=2).unsqueeze(1).to_broadcast([P, P, 2, 2])
+            nc.vector.tensor_tensor(
+                out=z_grouped[i, g][:].rearrange("p (n u e) -> p n u e", u=2, e=2), in0=values, in1=factor, op=ALU.mult
             )
 
-        def linear_form(i, w, h):
-            bank = psum.tile([P, HALF], F32, name="form", bufs=FORM_BANKS)
-            for g in range(GROUPS):
-                mx_pass(bank[:], z_codes[i, g][:], z_scales[i, g][:], w, h, g)
+        def quantize_z(i):
+            for g in BOTH:
+                z_codes[i, g] = work.tile([P, P], U32, name="z_codes", bufs=8, align_bytes=64)
+                z_scales[i, g] = work.tile([P, P], U8, name="z_scales", bufs=8, align_bytes=64)
+                nc.vector.quantize_mx(
+                    out=z_codes[i, g][:].bitcast(FP8X4), scales=z_scales[i, g][:], in_=z_grouped[i, g][:]
+                )
+
+        a2_plus_1, gain, x3 = {}, {}, {}
+
+        def product(codes, scales, i, w, h, tag):
+            bank = psum.tile([P, BANK], F32, name=tag, bufs=BANKS[tag])
+            for g in BOTH:
+                nc.tensor.matmul_mx(
+                    out=bank[:],
+                    lhsT=codes[i, g][:].bitcast(FP8X4),
+                    lhsT_scale=scales[i, g][:],
+                    rhs=w_codes[w, h][:, g, :].bitcast(FP8X4),
+                    rhs_scale=w_scales[w][SCALE_ROW[w] + 4 * g : P, h * BANK : (h + 1) * BANK],
+                    start=(g == BOTH[0]),
+                    stop=(g == BOTH[-1]),
+                )
             return bank
 
-        b2, y = {}, {}
-
         def step_a2(i, h):
-            bank = linear_form(i, "u2", h)
-            b2[i, h] = work.tile([P, HALF], F32, name="b2")
-            nc.scalar.activation(out=b2[i, h][:], in_=bank[:], func=ACT.Copy, bias=1.0)
+            bank = product(z_codes, z_scales, i, "u2", h, "form")
+            a2_plus_1[i, h] = work.tile([P, BANK], F32, name="a2_plus_1", bufs=2 * HEAD)
+            nc.scalar.activation(out=a2_plus_1[i, h][:], in_=bank[:], func=ACT.Copy, bias=1.0)
 
         def step_a3(i, h):
-            bank = linear_form(i, "u3", h)
-            y[i, h] = work.tile([P, HALF], F32, name="y")
+            bank = product(z_codes, z_scales, i, "u3", h, "form")
+            gain[i, h] = work.tile([P, BANK], F32, name="gain", bufs=2 * HEAD)
             nc.vector.scalar_tensor_tensor(
-                out=y[i, h][:], in0=bank[:], scalar=1.0, in1=b2[i, h][:], op0=ALU.add, op1=ALU.mult
+                out=gain[i, h][:], in0=bank[:], scalar=1.0, in1=a2_plus_1[i, h][:], op0=ALU.add, op1=ALU.mult
             )
 
         def step_x1(i, h):
-            bank = linear_form(i, "u1", h)
-            x3[i, h] = work.tile([P, HALF], BF16, name="x3", bufs=4, align_bytes=64)
+            bank = product(z_codes, z_scales, i, "u1", h, "form")
+            x3[i, h] = work.tile([P, BANK], BF16, name="x3", bufs=2 * HEAD, align_bytes=64)
             nc.vector.tensor_tensor(
                 out=x3[i, h][:].rearrange("n (u p e) -> n u p e", u=2, e=2),
                 in0=bank[:].rearrange("n (p u e) -> n u p e", u=2, e=2),
-                in1=y[i, h][:].rearrange("n (p u e) -> n u p e", u=2, e=2),
+                in1=gain[i, h][:].rearrange("n (p u e) -> n u p e", u=2, e=2),
                 op=ALU.mult,
             )
 
-        def turn_x3(i, groups):
+        x3_grouped, x3_codes, x3_scales, acc = {}, {}, {}, {}
+
+        def turn_x3(i, groups, tag="turned"):
             count = len(groups)
-            turned = psum.tile([P, 4, P], F32, name="turned", bufs=2)
+            bank = psum.tile([P, 4, P], F32, name=tag, bufs=BANKS[tag])
             for j, g in enumerate(groups):
                 words = x3[i, g][:].bitcast(F32)
                 for u in range(2):
-                    nc.tensor.transpose(turned[:, 2 * j + u, :], words[:, u * P : (u + 1) * P], ident[:])
-            grouped = work.tile([P, count * HALF], BF16, name="x3_grouped", align_bytes=64)
+                    nc.tensor.transpose(bank[:, 2 * j + u, :], words[:, u * P : (u + 1) * P], ident[:])
+            grouped = work.tile([P, count * GROUP], BF16, name="x3_grouped", align_bytes=64)
             x3_grouped[i, groups[0]] = grouped
             nc.scalar.copy(
                 out=grouped[:].bitcast(F32).rearrange("p (g n u) -> p g n u", g=count, u=2),
-                in_=turned[:, 0 : 2 * count, :].rearrange("p (g u) n -> p g n u", u=2),
+                in_=bank[:, 0 : 2 * count, :].rearrange("p (g u) n -> p g n u", u=2),
             )
 
         def quantize_x3(i, groups):
@@ -201,78 +209,79 @@ def tile_pinetccpthirddegreepolynomial_w8_kernel(
                 x3_codes[i, g] = codes[:, j * P : (j + 1) * P]
                 x3_scales[i, g] = scales[:, j * P : (j + 1) * P]
 
-        def project(i, tag, banks):
-            for h in range(2):
-                acc[i, h] = psum.tile([P, HALF], F32, name=tag, bufs=banks)
-                for g in range(GROUPS):
-                    mx_pass(acc[i, h][:], x3_codes[i, g], x3_scales[i, g], "c", h, g)
+        def project(i, tag="acc"):
+            for h in BOTH:
+                acc[i, h] = product(x3_codes, x3_scales, i, "c", h, tag)
 
         def finish(i, h):
-            res = work.tile([P, HALF], F32, name="res", bufs=6)
-            cols = slice(h * HALF, (h + 1) * HALF)
-            nc.vector.tensor_tensor(out=res[:], in0=acc[i, h][:], in1=beta_sb[:, cols], op=ALU.add)
+            res = work.tile([P, BANK], F32, name="res", bufs=6)
+            cols = slice(h * BANK, (h + 1) * BANK)
+            nc.vector.tensor_tensor(out=res[:], in0=acc[i, h][:], in1=beta_all[:, cols], op=ALU.add)
             nc.sync.dma_start(out=out_rows[:, i, cols], in_=res[:])
 
-        both = [0, 1]
-        widen_half(0, 0, nc.vector.tensor_copy)
-        widen_half(0, 1, nc.scalar.copy)
-        widen_half(1, 0, nc.vector.tensor_copy)
-        widen_half(1, 1, nc.scalar.copy)
-        widen_half(2, 0, nc.scalar.copy)
-        widen_half(2, 1, nc.scalar.copy)
-        turn_z(0, [0])
-        turn_z(0, [1])
-        turn_z(1, both, "acc")
-        turn_z(2, both, "acc")
-        for i in range(2):
-            for g in both:
+        for i in range(HEAD):
+            widen_group(i, 0, nc.vector.tensor_copy if i < HEAD - 1 else nc.scalar.copy)
+            widen_group(i, 1, nc.scalar.copy)
+        for g in BOTH:
+            turn_z(0, [g])
+        warm_up(2)
+        for i in range(1, HEAD):
+            turn_z(i, BOTH, "acc")
+        for i in range(HEAD):
+            for g in BOTH:
                 scale_z(i, g)
-            for g in both:
-                quantize_z(i, g)
-        step_a2(0, 0)
-        scale_z(2, 0)
-        step_a3(0, 0)
-        step_a2(1, 0)
-        scale_z(2, 1)
-        step_a3(1, 0)
-        step_x1(0, 0)
-        widen_z(3)
-        step_x1(1, 0)
-        step_a2(0, 1)
-        sort_z(3)
-        step_a2(1, 1)
-        step_a3(0, 1)
-        widen_z(4)
-        for g in both:
-            quantize_z(2, g)
-        step_x1(0, 1)
-        step_a3(1, 1)
-        step_x1(1, 1)
-        sort_z(4)
-        turn_x3(0, both)
-        turn_z(3, both)
-        for g in both:
-            scale_z(3, g)
+            quantize_z(i)
+
+        widen_z(HEAD)
+        for i in range(HEAD):
+            if i == HEAD - 1:
+                turn_z(HEAD, BOTH)
+            step_a2(i, 0)
+            if i == 0:
+                sort_z(HEAD)
+            step_a2(i, 1)
+        for g in BOTH:
+            scale_z(HEAD, g)
+        quantize_z(HEAD)
+        widen_z(HEAD + 1)
+        sort_z(HEAD + 1)
+        for h in BOTH:
+            for i in range(HEAD):
+                step_a3(i, h)
+        turn_z(HEAD + 1, BOTH)
+        widen_z(HEAD + 2)
+        sort_z(HEAD + 2)
+        scale_z(HEAD + 1, 0)
+        for i in range(HEAD):
+            for h in BOTH:
+                step_x1(i, h)
+        scale_z(HEAD + 1, 1)
+        turn_x3(0, BOTH)
+        turn_x3(1, BOTH, "acc")
+        quantize_x3(0, BOTH)
 
         last = TILES - 1
-        for i in range(2, last):
+        for i in range(HEAD, last):
             ahead = i + 2
             step_a2(i, 0)
             if ahead + 1 < TILES:
                 widen_z(ahead + 1)
             step_a3(i, 0)
-            if i == 2:
-                quantize_x3(0, both)
-                for g in both:
-                    quantize_z(3, g)
+            if i == HEAD:
+                quantize_x3(1, BOTH)
+                quantize_z(HEAD + 1)
             else:
                 finish(i - 3, 1)
             step_x1(i, 0)
-            turn_x3(i - 1, both)
+            if i == HEAD:
+                project(0)
+                for h in BOTH:
+                    finish(0, h)
+            turn_x3(i - 1, BOTH)
             if ahead < TILES:
-                turn_z(ahead, both)
+                turn_z(ahead, BOTH)
                 scale_z(ahead, 0)
-            quantize_x3(i - 1, both)
+            quantize_x3(i - 1, BOTH)
             if ahead < TILES:
                 scale_z(ahead, 1)
             step_a2(i, 1)
@@ -280,29 +289,29 @@ def tile_pinetccpthirddegreepolynomial_w8_kernel(
                 sort_z(ahead + 1)
             step_a3(i, 1)
             if ahead < TILES:
-                for g in both:
-                    quantize_z(ahead, g)
+                quantize_z(ahead)
             step_x1(i, 1)
-            project(i - 2, "acc", 2)
+            project(i - 2)
             finish(i - 2, 0)
+
         step_a2(last, 0)
         step_a3(last, 0)
         finish(last - 3, 1)
         step_x1(last, 0)
         step_a2(last, 1)
         step_a3(last, 1)
-        turn_x3(last - 1, both)
+        turn_x3(last - 1, BOTH)
         turn_x3(last, [0])
-        quantize_x3(last - 1, both)
+        quantize_x3(last - 1, BOTH)
         step_x1(last, 1)
-        project(last - 2, "acc", 2)
+        project(last - 2)
         quantize_x3(last, [0])
         finish(last - 2, 0)
         turn_x3(last, [1])
         finish(last - 2, 1)
-        project(last - 1, "form", FORM_BANKS)
+        project(last - 1, "form")
         quantize_x3(last, [1])
-        project(last, "form", FORM_BANKS)
+        project(last, "form")
         for i in (last - 1, last):
-            for h in range(2):
+            for h in BOTH:
                 finish(i, h)

from contextlib import ExitStack

import concourse.mybir as mybir
from concourse.masks import make_identity

N, D, R, O = 1024, 1024, 1024, 1024
FLOPS = 3 * 2 * N * D * R + 2 * N * R * O

F32 = mybir.dt.float32
BF16 = mybir.dt.bfloat16
U32 = mybir.dt.uint32
I32 = mybir.dt.int32
U8 = mybir.dt.uint8
FP8 = mybir.dt.float8_e4m3fn
FP8X4 = mybir.dt.float8_e4m3fn_x4
ALU = mybir.AluOpType
ACT = mybir.ActivationFunctionType

P = 128
TILES = N // P
GROUP = 512
BANK = 512
BOTH = [0, 1]
HEAD = 3
FORM_BANKS, ACC_BANKS, TURN_BANKS = 4, 2, 2
BANKS = {"form": FORM_BANKS, "acc": ACC_BANKS, "turned": TURN_BANKS}
SCALE_ROW = {"u2": 0, "u3": 8, "u1": 0, "c": 8}


def tile_pinetccpthirddegreepolynomial_w8_kernel(
    tc, z_bytes, z_scale, u1_words, u1_scales, u2_words, u2_scales, u3_words, u3_scales, c_words, c_scales, beta, out
):
    nc = tc.nc
    words_in = {"u1": u1_words, "u2": u2_words, "u3": u3_words, "c": c_words}
    scales_in = {"u1": u1_scales, "u2": u2_scales, "u3": u3_scales, "c": c_scales}
    z_rows = z_bytes.rearrange("(n i) k -> n i k", i=TILES)
    out_rows = out.rearrange("(n i) o -> n i o", i=TILES)

    with ExitStack() as ctx:
        keep = ctx.enter_context(tc.tile_pool(name="keep", bufs=1))
        work = ctx.enter_context(tc.tile_pool(name="work", bufs=3))
        psum = ctx.enter_context(tc.psum_pool(name="psum", bufs=1))
        ctx.enter_context(tc.manual_schedule())

        ident = keep.tile([P, P], F32, name="ident")
        make_identity(nc, ident[:])

        zeros = keep.tile([P, BANK], BF16, name="zeros", align_bytes=64)
        nc.vector.memset(zeros[:], 0.0)

        def warm_up(count):
            bank = psum.tile([P, BANK], F32, name="form", bufs=FORM_BANKS)
            for j in range(count):
                nc.tensor.matmul(bank[:], lhsT=zeros[:, 0:P], rhs=zeros[:], start=True, stop=True)

        warm_up(3)

        w_codes, w_scales, z_raw = {}, {}, {}
        for w in ("u2", "u3", "u1", "c"):
            w_scales[w] = keep.tile([P, R], U8, name="scales_" + w, align_bytes=64)
            nc.vector.memset(w_scales[w][:].bitcast(I32), 0)
            for h in BOTH:
                w_codes[w, h] = keep.tile([P, len(BOTH), BANK], U32, name="codes_%s_%d" % (w, h), align_bytes=64)

        def load_z(first, count):
            raw = keep.tile([P, count * D], U8, name="z_raw_%d" % first, align_bytes=64)
            nc.sync.dma_start(out=raw[:], in_=z_rows[:, first : first + count, :].rearrange("n i k -> n (i k)"))
            for j in range(count):
                z_raw[first + j] = raw[:, j * D : (j + 1) * D]

        def load_scales(w):
            for q in range(4):
                row = 32 * q + SCALE_ROW[w]
                nc.sync.dma_start(
                    out=w_scales[w][row : row + 8, :].bitcast(I32),
                    in_=scales_in[w][:, 4 * q : 4 * q + 4, :].bitcast(I32),
                )

        def load_codes(w, h):
            src = words_in[w].rearrange("g p n t -> p g (n t)")[:, :, 4 * BANK * h : 4 * BANK * (h + 1)]
            nc.sync.dma_start(out=w_codes[w, h][:].bitcast(I32), in_=src.bitcast(I32))

        z_factor = keep.tile([P, len(BOTH), 4], F32, name="z_factor")
        beta_all = keep.tile([P, O], BF16, name="beta_all")

        load_z(0, 1)
        load_z(1, HEAD - 1)
        nc.sync.dma_start(out=z_factor[:], in_=z_scale.rearrange("o (g p t) -> p (o g) t", p=P, t=4))
        for w, tile in (("u2", HEAD), ("u3", HEAD + 1)):
            load_scales(w)
            load_codes(w, 0)
            load_z(tile, 1)
            load_codes(w, 1)
        load_scales("u1")
        for h in BOTH:
            load_codes("u1", h)
        load_z(HEAD + 2, TILES - HEAD - 2)
        load_scales("c")
        for h in BOTH:
            load_codes("c", h)
        nc.sync.dma_start(out=beta_all[:], in_=beta.partition_broadcast(P))

        z_wide, z_words, z_turned, z_grouped, z_codes, z_scales = {}, {}, {}, {}, {}, {}

        def widen_group(i, g, copy):
            wide = work.tile([P, GROUP], BF16, name="z_first", bufs=2 * HEAD, align_bytes=64)
            copy(out=wide[:], in_=z_raw[i][:, g * GROUP : (g + 1) * GROUP].bitcast(FP8))
            for u in range(2):
                z_words[i, g, u] = wide[:].bitcast(F32)[:, u : GROUP // 2 : 2]

        def widen_z(i):
            z_wide[i] = work.tile([P, D], BF16, name="z_wide", bufs=2, align_bytes=64)
            nc.scalar.copy(out=z_wide[i][:], in_=z_raw[i].bitcast(FP8))

        def sort_z(i):
            ordered = work.tile([P, D // 2], F32, name="z_sorted", bufs=2, align_bytes=64)
            nc.scalar.copy(
                out=ordered[:].rearrange("n (g u p) -> n g u p", g=2, u=2),
                in_=z_wide[i][:].bitcast(F32).rearrange("n (g p u) -> n g u p", g=2, u=2),
            )
            for g in BOTH:
                for u in range(2):
                    z_words[i, g, u] = ordered[:, (2 * g + u) * P : (2 * g + u + 1) * P]

        def turn_z(i, groups, tag="turned"):
            bank = psum.tile([P, 4, P], F32, name=tag, bufs=BANKS[tag])
            for g in groups:
                z_turned[i, g] = bank
                for u in range(2):
                    nc.tensor.transpose(bank[:, 2 * g + u, :], z_words[i, g, u], ident[:])

        def scale_z(i, g):
            z_grouped[i, g] = work.tile([P, GROUP], BF16, name="z_grouped", bufs=4, align_bytes=64)
            values = z_turned[i, g][:].rearrange("p a n -> p (a n)").bitcast(BF16)
            values = values[:, g * GROUP : (g + 1) * GROUP].rearrange("p (u n e) -> p n u e", u=2, e=2)
            factor = z_factor[:, g, :].rearrange("p (u e) -> p u e", u=2).unsqueeze(1).to_broadcast([P, P, 2, 2])
            nc.vector.tensor_tensor(
                out=z_grouped[i, g][:].rearrange("p (n u e) -> p n u e", u=2, e=2), in0=values, in1=factor, op=ALU.mult
            )

        def quantize_z(i):
            for g in BOTH:
                z_codes[i, g] = work.tile([P, P], U32, name="z_codes", bufs=8, align_bytes=64)
                z_scales[i, g] = work.tile([P, P], U8, name="z_scales", bufs=8, align_bytes=64)
                nc.vector.quantize_mx(
                    out=z_codes[i, g][:].bitcast(FP8X4), scales=z_scales[i, g][:], in_=z_grouped[i, g][:]
                )

        a2_plus_1, gain, x3 = {}, {}, {}

        def product(codes, scales, i, w, h, tag):
            bank = psum.tile([P, BANK], F32, name=tag, bufs=BANKS[tag])
            for g in BOTH:
                nc.tensor.matmul_mx(
                    out=bank[:],
                    lhsT=codes[i, g][:].bitcast(FP8X4),
                    lhsT_scale=scales[i, g][:],
                    rhs=w_codes[w, h][:, g, :].bitcast(FP8X4),
                    rhs_scale=w_scales[w][SCALE_ROW[w] + 4 * g : P, h * BANK : (h + 1) * BANK],
                    start=(g == BOTH[0]),
                    stop=(g == BOTH[-1]),
                )
            return bank

        def step_a2(i, h):
            bank = product(z_codes, z_scales, i, "u2", h, "form")
            a2_plus_1[i, h] = work.tile([P, BANK], F32, name="a2_plus_1", bufs=2 * HEAD)
            nc.scalar.activation(out=a2_plus_1[i, h][:], in_=bank[:], func=ACT.Copy, bias=1.0)

        def step_a3(i, h):
            bank = product(z_codes, z_scales, i, "u3", h, "form")
            gain[i, h] = work.tile([P, BANK], F32, name="gain", bufs=2 * HEAD)
            nc.vector.scalar_tensor_tensor(
                out=gain[i, h][:], in0=bank[:], scalar=1.0, in1=a2_plus_1[i, h][:], op0=ALU.add, op1=ALU.mult
            )

        def step_x1(i, h):
            bank = product(z_codes, z_scales, i, "u1", h, "form")
            x3[i, h] = work.tile([P, BANK], BF16, name="x3", bufs=2 * HEAD, align_bytes=64)
            nc.vector.tensor_tensor(
                out=x3[i, h][:].rearrange("n (u p e) -> n u p e", u=2, e=2),
                in0=bank[:].rearrange("n (p u e) -> n u p e", u=2, e=2),
                in1=gain[i, h][:].rearrange("n (p u e) -> n u p e", u=2, e=2),
                op=ALU.mult,
            )

        x3_grouped, x3_codes, x3_scales, acc = {}, {}, {}, {}

        def turn_x3(i, groups, tag="turned"):
            count = len(groups)
            bank = psum.tile([P, 4, P], F32, name=tag, bufs=BANKS[tag])
            for j, g in enumerate(groups):
                words = x3[i, g][:].bitcast(F32)
                for u in range(2):
                    nc.tensor.transpose(bank[:, 2 * j + u, :], words[:, u * P : (u + 1) * P], ident[:])
            grouped = work.tile([P, count * GROUP], BF16, name="x3_grouped", align_bytes=64)
            x3_grouped[i, groups[0]] = grouped
            nc.scalar.copy(
                out=grouped[:].bitcast(F32).rearrange("p (g n u) -> p g n u", g=count, u=2),
                in_=bank[:, 0 : 2 * count, :].rearrange("p (g u) n -> p g n u", u=2),
            )

        def quantize_x3(i, groups):
            count = len(groups)
            codes = work.tile([P, count * P], U32, name="x3_codes", bufs=4, align_bytes=64)
            scales = work.tile([P, count * P], U8, name="x3_scales", bufs=4, align_bytes=64)
            nc.vector.quantize_mx(out=codes[:].bitcast(FP8X4), scales=scales[:], in_=x3_grouped[i, groups[0]][:])
            for j, g in enumerate(groups):
                x3_codes[i, g] = codes[:, j * P : (j + 1) * P]
                x3_scales[i, g] = scales[:, j * P : (j + 1) * P]

        def project(i, tag="acc"):
            for h in BOTH:
                acc[i, h] = product(x3_codes, x3_scales, i, "c", h, tag)

        def finish(i, h):
            res = work.tile([P, BANK], F32, name="res", bufs=6)
            cols = slice(h * BANK, (h + 1) * BANK)
            nc.vector.tensor_tensor(out=res[:], in0=acc[i, h][:], in1=beta_all[:, cols], op=ALU.add)
            nc.sync.dma_start(out=out_rows[:, i, cols], in_=res[:])

        for i in range(HEAD):
            widen_group(i, 0, nc.vector.tensor_copy if i < HEAD - 1 else nc.scalar.copy)
            widen_group(i, 1, nc.scalar.copy)
        for g in BOTH:
            turn_z(0, [g])
        warm_up(2)
        for i in range(1, HEAD):
            turn_z(i, BOTH, "acc")
        for i in range(HEAD):
            for g in BOTH:
                scale_z(i, g)
            quantize_z(i)

        widen_z(HEAD)
        for i in range(HEAD):
            if i == HEAD - 1:
                turn_z(HEAD, BOTH)
            step_a2(i, 0)
            if i == 0:
                sort_z(HEAD)
            step_a2(i, 1)
        for g in BOTH:
            scale_z(HEAD, g)
        quantize_z(HEAD)
        widen_z(HEAD + 1)
        sort_z(HEAD + 1)
        for h in BOTH:
            for i in range(HEAD):
                step_a3(i, h)
        turn_z(HEAD + 1, BOTH)
        widen_z(HEAD + 2)
        sort_z(HEAD + 2)
        scale_z(HEAD + 1, 0)
        for i in range(HEAD):
            for h in BOTH:
                step_x1(i, h)
        scale_z(HEAD + 1, 1)
        turn_x3(0, BOTH)
        turn_x3(1, BOTH, "acc")
        quantize_x3(0, BOTH)

        last = TILES - 1
        for i in range(HEAD, last):
            ahead = i + 2
            step_a2(i, 0)
            if ahead + 1 < TILES:
                widen_z(ahead + 1)
            step_a3(i, 0)
            if i == HEAD:
                quantize_x3(1, BOTH)
                quantize_z(HEAD + 1)
            else:
                finish(i - 3, 1)
            step_x1(i, 0)
            if i == HEAD:
                project(0)
                for h in BOTH:
                    finish(0, h)
            turn_x3(i - 1, BOTH)
            if ahead < TILES:
                turn_z(ahead, BOTH)
                scale_z(ahead, 0)
            quantize_x3(i - 1, BOTH)
            if ahead < TILES:
                scale_z(ahead, 1)
            step_a2(i, 1)
            if ahead + 1 < TILES:
                sort_z(ahead + 1)
            step_a3(i, 1)
            if ahead < TILES:
                quantize_z(ahead)
            step_x1(i, 1)
            project(i - 2)
            finish(i - 2, 0)

        step_a2(last, 0)
        step_a3(last, 0)
        finish(last - 3, 1)
        step_x1(last, 0)
        step_a2(last, 1)
        step_a3(last, 1)
        turn_x3(last - 1, BOTH)
        turn_x3(last, [0])
        quantize_x3(last - 1, BOTH)
        step_x1(last, 1)
        project(last - 2)
        quantize_x3(last, [0])
        finish(last - 2, 0)
        turn_x3(last, [1])
        finish(last - 2, 1)
        project(last - 1, "form")
        quantize_x3(last, [1])
        project(last, "form")
        for i in (last - 1, last):
            for h in BOTH:
                finish(i, h)
